import numpy as np
import ml_dtypes


def mxq(x, axis, fmt="e4m3"):
    dtype, down = {"e4m3": (ml_dtypes.float8_e4m3fn, 7), "e5m2": (ml_dtypes.float8_e5m2, 14)}[fmt]
    v = np.moveaxis(np.asarray(x, np.float32).astype(ml_dtypes.bfloat16).astype(np.float64), axis, -1)
    blocks = v.reshape(v.shape[:-1] + (-1, 32))
    amax = np.abs(blocks).max(-1, keepdims=True)
    byte = np.maximum(np.where(amax > 0, np.frexp(amax)[1] - 1 + 127, 0) - down, 1)
    scale = np.exp2(byte - 127.0)
    codes = (blocks / scale).astype(np.float32).astype(dtype).astype(np.float64)
    return np.moveaxis((codes * scale).reshape(v.shape), -1, axis)


WIDE = False


def mx_kscale(k):
    if not WIDE:
        return np.ones(k)
    levels = np.array([10, -10, 5, -5, 0])
    if k % 512:
        return np.exp2(np.random.permutation(np.resize(levels, k // 32))).repeat(32)
    a = np.empty((k // 512, 16))
    for p in range(k // 512):
        a[p, :8] = np.random.permutation(np.resize(levels, 8))
        for g in range(8):
            far = levels[np.abs(levels - a[p, g]) >= 10]
            a[p, g + 8] = far[np.random.randint(len(far))]
    return np.exp2(a.ravel()).repeat(32)


def f64(x):
    return np.asarray(x).astype(np.float64)


def striped8(idx):
    return np.asarray(idx).reshape(8, -1, 16).transpose(0, 2, 1).reshape(128, -1).astype(np.uint16)


def unstriped8(offs):
    return offs.reshape(8, 16, -1).transpose(0, 2, 1).reshape(8, -1).astype(np.int64)


def pick8(x, idx, run):
    r = np.arange(len(x))
    return x[r[:, None], idx[r % (8 * run) // run]]


E2M1 = np.array([0.0, 0.5, 1.0, 1.5, 2.0, 3.0, 4.0, 6.0, -0.0, -0.5, -1.0, -1.5, -2.0, -3.0, -4.0, -6.0])


def pack_weight(w, fmt):
    k, n = w.shape
    w = f64(np.asarray(w, np.float32).astype(ml_dtypes.bfloat16)).reshape(k // 32, 32, n)
    amax = np.abs(w).max(1)
    if fmt == "e4m3":
        byte = np.frexp(amax)[1] - 1 + 127 - 7
    else:
        mant, ex = np.frexp(amax / 6.0)
        byte = np.where(mant > 0.5, ex, ex - 1) + 127
    byte = np.clip(np.where(amax > 0, byte, 1), 1, 254)
    scaled = (w * np.exp2(127.0 - byte)[:, None, :]).reshape(k, n).astype(np.float32)
    by_word = np.ascontiguousarray(scaled.reshape(k // 512, 128, 4, n).transpose(0, 1, 3, 2))
    if fmt == "e4m3":
        words = by_word.astype(ml_dtypes.float8_e4m3fn).view(np.uint8)
    else:
        c = by_word.astype(ml_dtypes.float4_e2m1fn).view(np.uint8) & 0xF
        words = (c[..., 0::2] | (c[..., 1::2] << 4)).reshape(k // 512, 128, 2 * n)
    return np.ascontiguousarray(words), np.ascontiguousarray(byte.astype(np.uint8).reshape(k // 512, 16, n))


def unpack_weight(words, scales, fmt):
    g, _, n = scales.shape
    words = np.ascontiguousarray(words).reshape(g, 128, n, -1)
    if fmt == "e4m3":
        vals = words.view(ml_dtypes.float8_e4m3fn).astype(np.float64)
    else:
        nib = np.empty((g, 128, n, 4), np.uint8)
        nib[..., 0::2] = words & 0xF
        nib[..., 1::2] = words >> 4
        vals = E2M1[nib]
    vals = vals * np.repeat(np.exp2(scales.astype(np.float64) - 127.0), 8, axis=1)[..., None]
    return vals.transpose(0, 1, 3, 2).reshape(g * 512, n)


def sigmoid(v):
    return 1.0 / (1.0 + np.exp(-v))


D, T, I, Q = 512, 1024, 512, 128


def setup_inputs():
    n = np.random.standard_normal
    idx = np.stack([np.random.permutation(T)[:I] for _ in range(8)])
    idx2 = np.stack([np.random.permutation(T)[:I] for _ in range(8)])
    idx3 = np.stack([np.random.permutation(T)[:I] for _ in range(8)])
    idx4 = np.stack([np.random.permutation(T)[:I] for _ in range(8)])
    fd = mx_kscale(D)
    keysp = pack_weight(n((D, T)) / fd[:, None], "e4m3")
    return {
        "query": (n((D, Q)) * 0.9 / np.sqrt(D) * fd[:, None]).astype(np.float32),
        "keys_words": keysp[0],
        "keys_scales": keysp[1],
        "lam": (np.random.uniform(0.3, 0.9, (Q, 1))).astype(np.float32),
        "old": (1.0 * n((Q, T))).astype(np.float32),
        "share2": (np.random.uniform(0.4, 1.2, (Q, 1))).astype(np.float32),
        "offs": striped8(idx),
        "offs2": striped8(idx2),
        "offs3": striped8(idx3),
        "offs4": striped8(idx4),
    }


def reference(query, keys_words, keys_scales, lam, old, share2, offs, offs2, offs3, offs4):
    idx = unstriped8(offs)
    idx2 = unstriped8(offs2)
    idx3 = unstriped8(offs3)
    idx4 = unstriped8(offs4)
    keysu = unpack_weight(keys_words, keys_scales, "e4m3")
    queryq = mxq(f64(query), 0, "e4m3")
    a = queryq.T @ keysu
    s = pick8(a, idx, 16) + np.maximum(pick8(a, idx2, 16), pick8(a, idx3, 16)) * f64(lam)
    w = sigmoid(s)
    f1 = np.zeros((Q, T))
    f1[np.arange(Q)[:, None], idx[np.arange(Q) % 128 // 16]] = w
    f2 = np.zeros((Q, T))
    f2[np.arange(Q)[:, None], idx4[np.arange(Q) % 128 // 16]] = w
    y = f64(old) + f1 + f2 * f64(share2)
    return y

@@ -1,0 +1,165 @@
+import concourse.mybir as mybir
+
+D, T, SLOTS, Q = 512, 1024, 512, 128
+FLOPS = 2 * D * Q * T
+
+F32 = mybir.dt.float32
+BF16 = mybir.dt.bfloat16
+I32 = mybir.dt.int32
+U32 = mybir.dt.uint32
+U16 = mybir.dt.uint16
+U8 = mybir.dt.uint8
+FP8X4 = mybir.dt.float8_e4m3fn_x4
+ALU = mybir.AluOpType
+ACT = mybir.ActivationFunctionType
+
+P = 128
+PACK = 4
+GROUP = 16
+HALF = SLOTS // 2
+N_MM = 256
+N_OUT = 256
+
+
+def tile_attend_lookahead_lean_twiceput_heads_kernel(
+    tc, query, keys_words, keys_scales, lam, old, share2, offs, offs2, offs3, offs4, out
+):
+    nc = tc.nc
+    with tc.tile_pool(name="sb", bufs=1) as sb, tc.psum_pool(name="ps", bufs=1) as ps:
+        q_raw = sb.tile([P, PACK, Q], F32, name="q_raw")
+        nc.sync.dma_start(out=q_raw[:], in_=query.rearrange("(p j) q -> p j q", j=PACK))
+
+        k_scales = sb.tile([P, T], U8, name="k_scales", align_bytes=64)
+        nc.vector.memset(k_scales[:].bitcast(I32), 0)
+        for quad in range(4):
+            nc.scalar.dma_start(
+                out=k_scales[32 * quad : 32 * quad + 4, :].bitcast(I32),
+                in_=keys_scales[0, 4 * quad : 4 * quad + 4, :].bitcast(I32),
+            )
+        words_hbm = keys_words[0].rearrange("p n t -> p (n t)").bitcast(I32)
+        k_words = []
+        for h in range(2):
+            half_words = sb.tile([P, T // 2], I32, name=f"k_words{h}", align_bytes=64)
+            nc.sync.dma_start(out=half_words[:], in_=words_hbm[:, h * (T // 2) : (h + 1) * (T // 2)])
+            k_words.append(half_words)
+
+        lists = {}
+        for name, src in (("o3", offs3), ("o2", offs2), ("o1", offs)):
+            lists[name] = sb.tile([P, SLOTS // GROUP], U16, name=name)
+            nc.sync.dma_start(lists[name][:], src)
+        lam_col = sb.tile([P, 1], F32, name="lam_col")
+        nc.sync.dma_start(out=lam_col[:], in_=lam)
+        lists["o4"] = sb.tile([P, SLOTS // GROUP], U16, name="o4")
+        nc.sync.dma_start(lists["o4"][:], offs4)
+        share_col = sb.tile([P, 1], F32, name="share_col")
+        nc.sync.dma_start(out=share_col[:], in_=share2)
+        old_sb = sb.tile([P, T], F32, name="old_sb")
+        nc.sync.dma_start(out=old_sb[:], in_=old)
+
+        f1 = sb.tile([P, T], F32, name="f1")
+        f2 = sb.tile([P, T], F32, name="f2")
+        nc.vector.memset(f1[:], 0.0)
+        warm = sb.tile([P, 1], F32, name="warm")
+        nc.vector.memset(warm[:], 0.0)
+        warm_out = sb.tile([P, 1], F32, name="warm_out")
+        nc.scalar.activation(warm_out[:], warm[:], ACT.Sigmoid)
+        nc.vector.memset(f2[:], 0.0)
+
+        def entries(name, first, last):
+            return lists[name][:, first // GROUP : last // GROUP]
+
+        q_bf = sb.tile([P, Q, PACK], BF16, name="q_bf", align_bytes=64)
+        q_codes = sb.tile([P, Q], U32, name="q_codes", align_bytes=64)
+        q_scales = sb.tile([P, Q], U8, name="q_scales", align_bytes=64)
+        halves = [slice(0, Q // 2), slice(Q // 2, Q)]
+        for cols in halves:
+            nc.vector.tensor_copy(out=q_bf[:, cols, :], in_=q_raw[:, :, cols].rearrange("p j q -> p q j"))
+        for cols in halves:
+            nc.vector.quantize_mx(
+                out=q_codes[:, cols].bitcast(FP8X4),
+                scales=q_scales[:, cols],
+                in_=q_bf[:, cols, :].rearrange("p q j -> p (q j)"),
+            )
+
+        a = sb.tile([P, T], F32, name="a")
+        for c, (start, width) in enumerate([(0, 256), (256, 256), (512, 256), (768, 128), (896, 128)]):
+            cols = slice(start, start + width)
+            h, first = divmod(start, T // 2)
+            bank = ps.tile([P, width], F32, name=f"bank{c}")
+            nc.tensor.matmul_mx(
+                out=bank[:],
+                lhsT=q_codes[:].bitcast(FP8X4),
+                lhsT_scale=q_scales[:],
+                rhs=k_words[h][:, first : first + width].bitcast(FP8X4),
+                rhs_scale=k_scales[:, cols],
+                start=True,
+                stop=True,
+            )
+            if c % 2 == 0:
+                nc.vector.tensor_copy(out=a[:, cols], in_=bank[:])
+            else:
+                nc.scalar.activation(a[:, cols], bank[:], ACT.Copy)
+
+        g1 = [sb.tile([P, HALF], F32, name=f"g1_{h}") for h in range(2)]
+        g2 = [sb.tile([P, HALF], F32, name=f"g2_{h}") for h in range(2)]
+        g3 = [sb.tile([P, HALF], F32, name=f"g3_{h}") for h in range(2)]
+        m = [g1[1], sb.tile([P, HALF], F32, name="m_1")]
+        s = sb.tile([P, SLOTS], F32, name="s")
+        w = sb.tile([P, SLOTS], F32, name="w")
+        w2 = sb.tile([P, SLOTS], F32, name="w2")
+
+        def vgather(dst, name, h):
+            nc.vector.tensor_copy(dst[:], a[:].indirect(entries(name, h * HALF, (h + 1) * HALF)))
+
+        def sgather(dst, name, h):
+            nc.scalar.activation(dst[:], a[:].indirect(entries(name, h * HALF, (h + 1) * HALF)), ACT.Copy)
+
+        def larger(first, last):
+            h, at = divmod(first, HALF)
+            cols = slice(at, at + last - first)
+            nc.vector.tensor_tensor(m[h][:, cols], g2[h][:, cols], g3[h][:, cols], ALU.max)
+
+        def score(first, last):
+            h, at = divmod(first, HALF)
+            cols = slice(at, at + last - first)
+            nc.vector.scalar_tensor_tensor(s[:, first:last], m[h][:, cols], lam_col[:], g1[h][:, cols], ALU.mult, ALU.add)
+
+        def weigh(first, last):
+            nc.scalar.activation(w[:, first:last], s[:, first:last], ACT.Sigmoid)
+
+        def shared(first, last):
+            nc.scalar.activation(w2[:, first:last], w[:, first:last], ACT.Copy, scale=share_col[:])
+
+        def put(window, name, src, first, last):
+            nc.vector.tensor_copy(window[:].indirect(entries(name, first, last)), src[:, first:last])
+
+        sgather(g3[0], "o3", 0)
+        vgather(g2[0], "o2", 0)
+        sgather(g1[0], "o1", 0)
+        vgather(g2[1], "o2", 1)
+        larger(0, 128)
+        larger(128, 256)
+        sgather(g3[1], "o3", 1)
+        score(0, 128)
+        score(128, 256)
+        larger(256, 512)
+        weigh(0, 128)
+        weigh(128, 256)
+        sgather(g1[1], "o1", 1)
+        put(f1, "o1", w, 0, 128)
+        score(256, 512)
+        shared(0, 128)
+        weigh(256, 512)
+        put(f2, "o4", w2, 0, 128)
+        shared(128, 512)
+        put(f1, "o1", w, 128, 512)
+        put(f2, "o4", w2, 128, 512)
+
+        for c in range(T // N_OUT):
+            cols = slice(c * N_OUT, (c + 1) * N_OUT)
+            part = sb.tile([P, N_OUT], F32, name=f"part{c}")
+            nc.gpsimd.tensor_tensor(part[:], old_sb[:, cols], f1[:, cols], ALU.add)
+            res = sb.tile([P, N_OUT], F32, name=f"res{c}")
+            nc.vector.tensor_tensor(res[:], f2[:, cols], part[:], ALU.add)
+            queue = nc.sync if c % 2 == 0 else nc.scalar
+            queue.dma_start(out=out[:, cols], in_=res[:])

@@ -1,4 +1,5 @@
 import concourse.mybir as mybir
+from concourse.masks import make_identity
 
 D, T, SLOTS, Q = 512, 1024, 512, 128
 FLOPS = 2 * D * Q * T
@@ -81,13 +82,16 @@ def tile_attend_lookahead_lean_twiceput_heads_kernel(
                 in_=q_bf[:, cols, :].rearrange("p q j -> p (q j)"),
             )
 
+        ident = sb.tile([P, P], F32, name="ident")
+        make_identity(nc, ident[:])
+        banks = [ps.tile([P, 512], F32, name=f"bank{b}") for b in range(8)]
         a = sb.tile([P, T], F32, name="a")
         for c, (start, width) in enumerate([(0, 256), (256, 256), (512, 256), (768, 128), (896, 128)]):
             cols = slice(start, start + width)
             h, first = divmod(start, T // 2)
-            bank = ps.tile([P, width], F32, name=f"bank{c}")
+            bank = banks[c][:, 0:width]
             nc.tensor.matmul_mx(
-                out=bank[:],
+                out=bank,
                 lhsT=q_codes[:].bitcast(FP8X4),
                 lhsT_scale=q_scales[:],
                 rhs=k_words[h][:, first : first + width].bitcast(FP8X4),
@@ -96,9 +100,12 @@ def tile_attend_lookahead_lean_twiceput_heads_kernel(
                 stop=True,
             )
             if c % 2 == 0:
-                nc.vector.tensor_copy(out=a[:, cols], in_=bank[:])
+                nc.vector.tensor_copy(out=a[:, cols], in_=bank)
             else:
-                nc.scalar.activation(a[:, cols], bank[:], ACT.Copy)
+                nc.scalar.activation(a[:, cols], bank, ACT.Copy)
+
+        for j in range(8):
+            nc.tensor.matmul(banks[j][:, 0:P], old_sb[:, j * P : (j + 1) * P], ident[:], start=True, stop=False, is_transpose=True)
 
         g1 = [sb.tile([P, HALF], F32, name=f"g1_{h}") for h in range(2)]
         g2 = [sb.tile([P, HALF], F32, name=f"g2_{h}") for h in range(2)]
@@ -155,11 +162,18 @@ def tile_attend_lookahead_lean_twiceput_heads_kernel(
         put(f1, "o1", w, 128, 512)
         put(f2, "o4", w2, 128, 512)
 
+        turned = sb.tile([P, T], F32, name="turned")
+        for j in range(8):
+            cols = slice(j * P, (j + 1) * P)
+            nc.tensor.matmul(banks[j][:, 0:P], f1[:, cols], ident[:], start=False, stop=True, is_transpose=True)
+            nc.scalar.activation(turned[:, cols], banks[j][:, 0:P], ACT.Copy)
         for c in range(T // N_OUT):
             cols = slice(c * N_OUT, (c + 1) * N_OUT)
-            part = sb.tile([P, N_OUT], F32, name=f"part{c}")
-            nc.gpsimd.tensor_tensor(part[:], old_sb[:, cols], f1[:, cols], ALU.add)
+            part = banks[2 * c][:, N_OUT : 2 * N_OUT]
+            for u in range(2):
+                j = 2 * c + u
+                nc.tensor.transpose(part[:, u * P : (u + 1) * P], turned[:, j * P : (j + 1) * P], ident[:])
             res = sb.tile([P, N_OUT], F32, name=f"res{c}")
-            nc.vector.tensor_tensor(res[:], f2[:, cols], part[:], ALU.add)
+            nc.vector.tensor_tensor(res[:], part, f2[:, cols], ALU.add)
             queue = nc.sync if c % 2 == 0 else nc.scalar
             queue.dma_start(out=out[:, cols], in_=res[:])

@@ -74,7 +74,10 @@ def tile_attend_lookahead_lean_twiceput_heads_kernel(
         q_scales = sb.tile([P, Q], U8, name="q_scales", align_bytes=64)
         halves = [slice(0, Q // 2), slice(Q // 2, Q)]
         for cols in halves:
-            nc.vector.tensor_copy(out=q_bf[:, cols, :], in_=q_raw[:, :, cols].rearrange("p j q -> p q j"))
+            nc.vector.tensor_copy(
+                out=q_bf[:, cols, :].rearrange("p (c i) j -> p c j i", i=4),
+                in_=q_raw[:, :, cols].rearrange("p j (c i) -> p c j i", i=4),
+            )
         for cols in halves:
             nc.vector.quantize_mx(
                 out=q_codes[:, cols].bitcast(FP8X4),
@@ -104,7 +107,7 @@ def tile_attend_lookahead_lean_twiceput_heads_kernel(
             else:
                 nc.scalar.activation(a[:, cols], bank, ACT.Copy)
 
-        for j in range(8):
+        for j in range(4, 8):
             nc.tensor.matmul(banks[j][:, 0:P], old_sb[:, j * P : (j + 1) * P], ident[:], start=True, stop=False, is_transpose=True)
 
         g1 = [sb.tile([P, HALF], F32, name=f"g1_{h}") for h in range(2)]
@@ -113,7 +116,6 @@ def tile_attend_lookahead_lean_twiceput_heads_kernel(
         m = [g1[1], sb.tile([P, HALF], F32, name="m_1")]
         s = sb.tile([P, SLOTS], F32, name="s")
         w = sb.tile([P, SLOTS], F32, name="w")
-        w2 = sb.tile([P, SLOTS], F32, name="w2")
 
         def vgather(dst, name, h):
             nc.vector.tensor_copy(dst[:], a[:].indirect(entries(name, h * HALF, (h + 1) * HALF)))
@@ -134,9 +136,6 @@ def tile_attend_lookahead_lean_twiceput_heads_kernel(
         def weigh(first, last):
             nc.scalar.activation(w[:, first:last], s[:, first:last], ACT.Sigmoid)
 
-        def shared(first, last):
-            nc.scalar.activation(w2[:, first:last], w[:, first:last], ACT.Copy, scale=share_col[:])
-
         def put(window, name, src, first, last):
             nc.vector.tensor_copy(window[:].indirect(entries(name, first, last)), src[:, first:last])
 
@@ -153,27 +152,32 @@ def tile_attend_lookahead_lean_twiceput_heads_kernel(
         weigh(0, 128)
         weigh(128, 256)
         sgather(g1[1], "o1", 1)
-        put(f1, "o1", w, 0, 128)
-        score(256, 512)
-        shared(0, 128)
+        leaned = sb.tile([P, HALF], F32, name="leaned")
+        nc.gpsimd.tensor_scalar(leaned[:], m[1][:], lam_col[:], 0.0, ALU.mult, ALU.add)
+        nc.gpsimd.tensor_tensor(s[:, HALF:], leaned[:], g1[1][:], ALU.add)
         weigh(256, 512)
-        put(f2, "o4", w2, 0, 128)
-        shared(128, 512)
+        put(f1, "o1", w, 0, 128)
+        put(f2, "o4", w, 0, 256)
         put(f1, "o1", w, 128, 512)
-        put(f2, "o4", w2, 128, 512)
+        put(f2, "o4", w, 256, 512)
 
         turned = sb.tile([P, T], F32, name="turned")
-        for j in range(8):
+        for j in range(4, 8):
             cols = slice(j * P, (j + 1) * P)
             nc.tensor.matmul(banks[j][:, 0:P], f1[:, cols], ident[:], start=False, stop=True, is_transpose=True)
             nc.scalar.activation(turned[:, cols], banks[j][:, 0:P], ACT.Copy)
         for c in range(T // N_OUT):
             cols = slice(c * N_OUT, (c + 1) * N_OUT)
-            part = banks[2 * c][:, N_OUT : 2 * N_OUT]
-            for u in range(2):
-                j = 2 * c + u
-                nc.tensor.transpose(part[:, u * P : (u + 1) * P], turned[:, j * P : (j + 1) * P], ident[:])
+            if c < 2:
+                part_sb = sb.tile([P, N_OUT], F32, name=f"part{c}")
+                part = part_sb[:]
+                nc.gpsimd.tensor_tensor(part, old_sb[:, cols], f1[:, cols], ALU.add)
+            else:
+                part = banks[c - 2][:, 0:N_OUT]
+                for u in range(2):
+                    j = 2 * c + u
+                    nc.tensor.transpose(part[:, u * P : (u + 1) * P], turned[:, j * P : (j + 1) * P], ident[:])
             res = sb.tile([P, N_OUT], F32, name=f"res{c}")
-            nc.vector.tensor_tensor(res[:], part, f2[:, cols], ALU.add)
+            nc.vector.scalar_tensor_tensor(res[:], f2[:, cols], share_col[:], part, ALU.mult, ALU.add)
             queue = nc.sync if c % 2 == 0 else nc.scalar
             queue.dma_start(out=out[:, cols], in_=res[:])

@@ -16,10 +16,17 @@ ACT = mybir.ActivationFunctionType
 
 P = 128
 PACK = 4
-GROUP = 16
+QUADRANT = 32
+SCALE_ROWS = 4
+HEAD = 16
+BANKS, BANK_COLUMNS = 8, 512
+PLANES = 4
+PLANE = T // PLANES
 HALF = SLOTS // 2
-N_MM = 256
-N_OUT = 256
+QUARTER = SLOTS // 4
+MATMULS = [(0, 256), (256, 256), (512, 256), (768, 128), (896, 128)]
+CHUNK = 256
+GPSIMD_COLUMNS = T // 2
 
 
 def tile_attend_lookahead_lean_twiceput_heads_kernel(
@@ -30,28 +37,30 @@ def tile_attend_lookahead_lean_twiceput_heads_kernel(
         q_raw = sb.tile([P, PACK, Q], F32, name="q_raw")
         nc.sync.dma_start(out=q_raw[:], in_=query.rearrange("(p j) q -> p j q", j=PACK))
 
-        k_scales = sb.tile([P, T], U8, name="k_scales", align_bytes=64)
+        k_scales = sb.tile([P, PLANE], U8, name="k_scales", align_bytes=64)
         nc.vector.memset(k_scales[:].bitcast(I32), 0)
-        for quad in range(4):
-            nc.scalar.dma_start(
-                out=k_scales[32 * quad : 32 * quad + 4, :].bitcast(I32),
-                in_=keys_scales[0, 4 * quad : 4 * quad + 4, :].bitcast(I32),
-            )
         words_hbm = keys_words[0].rearrange("p n t -> p (n t)").bitcast(I32)
-        k_words = []
-        for h in range(2):
-            half_words = sb.tile([P, T // 2], I32, name=f"k_words{h}", align_bytes=64)
-            nc.sync.dma_start(out=half_words[:], in_=words_hbm[:, h * (T // 2) : (h + 1) * (T // 2)])
-            k_words.append(half_words)
+        k_words = [sb.tile([P, T // 2], I32, name=f"k_words{h}", align_bytes=64) for h in range(2)]
+        nc.sync.dma_start(out=k_words[0][:], in_=words_hbm[:, 0 : T // 2])
+        for quad in range(P // QUADRANT):
+            rows = keys_scales[0, SCALE_ROWS * quad : SCALE_ROWS * (quad + 1), :].bitcast(I32)
+            nc.sync.dma_start(
+                out=k_scales[QUADRANT * quad : QUADRANT * quad + PLANES * SCALE_ROWS, :].bitcast(I32),
+                in_=rows.rearrange("j (c n) -> c j n", c=PLANES),
+            )
+        nc.sync.dma_start(out=k_words[1][:], in_=words_hbm[:, T // 2 : T])
 
-        lists = {}
-        for name, src in (("o3", offs3), ("o2", offs2), ("o1", offs)):
-            lists[name] = sb.tile([P, SLOTS // GROUP], U16, name=name)
-            nc.sync.dma_start(lists[name][:], src)
+        def load_list(name, src):
+            entries = sb.tile([P, SLOTS // HEAD], U16, name=name)
+            nc.sync.dma_start(entries[:], src)
+            return entries
+
+        list1 = load_list("list1", offs)
+        list3 = load_list("list3", offs3)
+        list2 = load_list("list2", offs2)
         lam_col = sb.tile([P, 1], F32, name="lam_col")
         nc.sync.dma_start(out=lam_col[:], in_=lam)
-        lists["o4"] = sb.tile([P, SLOTS // GROUP], U16, name="o4")
-        nc.sync.dma_start(lists["o4"][:], offs4)
+        list4 = load_list("list4", offs4)
         share_col = sb.tile([P, 1], F32, name="share_col")
         nc.sync.dma_start(out=share_col[:], in_=share2)
         old_sb = sb.tile([P, T], F32, name="old_sb")
@@ -60,124 +69,122 @@ def tile_attend_lookahead_lean_twiceput_heads_kernel(
         f1 = sb.tile([P, T], F32, name="f1")
         f2 = sb.tile([P, T], F32, name="f2")
         nc.vector.memset(f1[:], 0.0)
-        warm = sb.tile([P, 1], F32, name="warm")
-        nc.vector.memset(warm[:], 0.0)
+        warm_in = sb.tile([P, 1], F32, name="warm_in")
+        nc.vector.memset(warm_in[:], 0.0)
         warm_out = sb.tile([P, 1], F32, name="warm_out")
-        nc.scalar.activation(warm_out[:], warm[:], ACT.Sigmoid)
+        nc.scalar.activation(warm_out[:], warm_in[:], ACT.Sigmoid)
         nc.vector.memset(f2[:], 0.0)
-
-        def entries(name, first, last):
-            return lists[name][:, first // GROUP : last // GROUP]
 
         q_bf = sb.tile([P, Q, PACK], BF16, name="q_bf", align_bytes=64)
         q_codes = sb.tile([P, Q], U32, name="q_codes", align_bytes=64)
         q_scales = sb.tile([P, Q], U8, name="q_scales", align_bytes=64)
-        halves = [slice(0, Q // 2), slice(Q // 2, Q)]
-        for cols in halves:
+        q_halves = [slice(0, Q // 2), slice(Q // 2, Q)]
+        for q_cols in q_halves:
             nc.vector.tensor_copy(
-                out=q_bf[:, cols, :].rearrange("p (c i) j -> p c j i", i=4),
-                in_=q_raw[:, :, cols].rearrange("p j (c i) -> p c j i", i=4),
+                out=q_bf[:, q_cols, :].rearrange("p (c i) j -> p c j i", i=4),
+                in_=q_raw[:, :, q_cols].rearrange("p j (c i) -> p c j i", i=4),
             )
-        for cols in halves:
+        for q_cols in q_halves:
             nc.vector.quantize_mx(
-                out=q_codes[:, cols].bitcast(FP8X4),
-                scales=q_scales[:, cols],
-                in_=q_bf[:, cols, :].rearrange("p q j -> p (q j)"),
+                out=q_codes[:, q_cols].bitcast(FP8X4),
+                scales=q_scales[:, q_cols],
+                in_=q_bf[:, q_cols, :].rearrange("p q j -> p (q j)"),
             )
 
         ident = sb.tile([P, P], F32, name="ident")
         make_identity(nc, ident[:])
-        banks = [ps.tile([P, 512], F32, name=f"bank{b}") for b in range(8)]
+        banks = [ps.tile([P, BANK_COLUMNS], F32, name=f"bank{b}") for b in range(BANKS)]
         a = sb.tile([P, T], F32, name="a")
-        for c, (start, width) in enumerate([(0, 256), (256, 256), (512, 256), (768, 128), (896, 128)]):
-            cols = slice(start, start + width)
-            h, first = divmod(start, T // 2)
-            bank = banks[c][:, 0:width]
+        for b, (token, count) in enumerate(MATMULS):
+            words_half, word = divmod(token, T // 2)
+            plane, plane_col = divmod(token, PLANE)
+            sums = banks[b][:, 0:count]
             nc.tensor.matmul_mx(
-                out=bank,
+                out=sums,
                 lhsT=q_codes[:].bitcast(FP8X4),
                 lhsT_scale=q_scales[:],
-                rhs=k_words[h][:, first : first + width].bitcast(FP8X4),
-                rhs_scale=k_scales[:, cols],
+                rhs=k_words[words_half][:, word : word + count].bitcast(FP8X4),
+                rhs_scale=k_scales[SCALE_ROWS * plane : P, plane_col : plane_col + count],
                 start=True,
                 stop=True,
             )
-            if c % 2 == 0:
-                nc.vector.tensor_copy(out=a[:, cols], in_=bank)
+            if b % 2 == 0:
+                nc.vector.tensor_copy(out=a[:, token : token + count], in_=sums)
             else:
-                nc.scalar.activation(a[:, cols], bank, ACT.Copy)
+                nc.scalar.activation(a[:, token : token + count], sums, ACT.Copy)
 
-        for j in range(4, 8):
-            nc.tensor.matmul(banks[j][:, 0:P], old_sb[:, j * P : (j + 1) * P], ident[:], start=True, stop=False, is_transpose=True)
+        tensor_blocks = range(GPSIMD_COLUMNS // P, T // P)
+        for j in tensor_blocks:
+            nc.tensor.matmul(
+                banks[j][:, 0:P], old_sb[:, j * P : (j + 1) * P], ident[:], start=True, stop=False, is_transpose=True
+            )
 
         g1 = [sb.tile([P, HALF], F32, name=f"g1_{h}") for h in range(2)]
         g2 = [sb.tile([P, HALF], F32, name=f"g2_{h}") for h in range(2)]
         g3 = [sb.tile([P, HALF], F32, name=f"g3_{h}") for h in range(2)]
-        m = [g1[1], sb.tile([P, HALF], F32, name="m_1")]
+        larger = [g1[1], g1[0]]
         s = sb.tile([P, SLOTS], F32, name="s")
         w = sb.tile([P, SLOTS], F32, name="w")
 
-        def vgather(dst, name, h):
-            nc.vector.tensor_copy(dst[:], a[:].indirect(entries(name, h * HALF, (h + 1) * HALF)))
+        def offsets(entries, first, last):
+            return entries[:, first // HEAD : last // HEAD]
 
-        def sgather(dst, name, h):
-            nc.scalar.activation(dst[:], a[:].indirect(entries(name, h * HALF, (h + 1) * HALF)), ACT.Copy)
-
-        def larger(first, last):
-            h, at = divmod(first, HALF)
-            cols = slice(at, at + last - first)
-            nc.vector.tensor_tensor(m[h][:, cols], g2[h][:, cols], g3[h][:, cols], ALU.max)
-
-        def score(first, last):
-            h, at = divmod(first, HALF)
-            cols = slice(at, at + last - first)
-            nc.vector.scalar_tensor_tensor(s[:, first:last], m[h][:, cols], lam_col[:], g1[h][:, cols], ALU.mult, ALU.add)
+        def looked_up(entries, h):
+            return a[:].indirect(offsets(entries, h * HALF, (h + 1) * HALF))
 
         def weigh(first, last):
             nc.scalar.activation(w[:, first:last], s[:, first:last], ACT.Sigmoid)
 
-        def put(window, name, src, first, last):
-            nc.vector.tensor_copy(window[:].indirect(entries(name, first, last)), src[:, first:last])
+        def put(window, entries, first, last):
+            nc.vector.tensor_copy(window[:].indirect(offsets(entries, first, last)), w[:, first:last])
 
-        sgather(g3[0], "o3", 0)
-        vgather(g2[0], "o2", 0)
-        sgather(g1[0], "o1", 0)
-        vgather(g2[1], "o2", 1)
-        larger(0, 128)
-        larger(128, 256)
-        sgather(g3[1], "o3", 1)
-        score(0, 128)
-        score(128, 256)
-        larger(256, 512)
-        weigh(0, 128)
-        weigh(128, 256)
-        sgather(g1[1], "o1", 1)
+        quarters = [slice(0, QUARTER), slice(QUARTER, HALF)]
+        nc.scalar.activation(g3[0][:], looked_up(list3, 0), ACT.Copy)
+        nc.vector.tensor_copy(g2[0][:], looked_up(list2, 0))
+        nc.scalar.activation(g1[0][:], looked_up(list1, 0), ACT.Copy)
+        nc.vector.tensor_copy(g2[1][:], looked_up(list2, 1))
+        for slots in quarters:
+            nc.vector.tensor_tensor(larger[0][:, slots], g2[0][:, slots], g3[0][:, slots], ALU.max)
+        nc.scalar.activation(g3[1][:], looked_up(list3, 1), ACT.Copy)
+        for slots in quarters:
+            nc.vector.scalar_tensor_tensor(
+                s[:, slots], larger[0][:, slots], lam_col[:], g1[0][:, slots], ALU.mult, ALU.add
+            )
+        nc.vector.tensor_tensor(larger[1][:], g2[1][:], g3[1][:], ALU.max)
+        for slots in quarters:
+            weigh(slots.start, slots.stop)
+        nc.scalar.activation(g1[1][:], looked_up(list1, 1), ACT.Copy)
         leaned = sb.tile([P, HALF], F32, name="leaned")
-        nc.gpsimd.tensor_scalar(leaned[:], m[1][:], lam_col[:], 0.0, ALU.mult, ALU.add)
+        nc.gpsimd.tensor_scalar(leaned[:], larger[1][:], lam_col[:], 0.0, ALU.mult, ALU.add)
         nc.gpsimd.tensor_tensor(s[:, HALF:], leaned[:], g1[1][:], ALU.add)
-        weigh(256, 512)
-        put(f1, "o1", w, 0, 128)
-        put(f2, "o4", w, 0, 256)
-        put(f1, "o1", w, 128, 512)
-        put(f2, "o4", w, 256, 512)
+        weigh(HALF, SLOTS)
 
-        turned = sb.tile([P, T], F32, name="turned")
-        for j in range(4, 8):
-            cols = slice(j * P, (j + 1) * P)
-            nc.tensor.matmul(banks[j][:, 0:P], f1[:, cols], ident[:], start=False, stop=True, is_transpose=True)
-            nc.scalar.activation(turned[:, cols], banks[j][:, 0:P], ACT.Copy)
-        for c in range(T // N_OUT):
-            cols = slice(c * N_OUT, (c + 1) * N_OUT)
-            if c < 2:
-                part_sb = sb.tile([P, N_OUT], F32, name=f"part{c}")
+        put(f1, list1, 0, QUARTER)
+        put(f2, list4, 0, HALF)
+        put(f1, list1, QUARTER, SLOTS)
+        put(f2, list4, HALF, SLOTS)
+
+        turned = sb.tile([P, T - GPSIMD_COLUMNS], F32, name="turned")
+        for j in tensor_blocks:
+            nc.tensor.matmul(
+                banks[j][:, 0:P], f1[:, j * P : (j + 1) * P], ident[:], start=False, stop=True, is_transpose=True
+            )
+            at = j * P - GPSIMD_COLUMNS
+            nc.scalar.activation(turned[:, at : at + P], banks[j][:, 0:P], ACT.Copy)
+        for c in range(T // CHUNK):
+            cols = slice(c * CHUNK, (c + 1) * CHUNK)
+            if cols.start < GPSIMD_COLUMNS:
+                part_sb = sb.tile([P, CHUNK], F32, name=f"part{c}")
                 part = part_sb[:]
                 nc.gpsimd.tensor_tensor(part, old_sb[:, cols], f1[:, cols], ALU.add)
             else:
-                part = banks[c - 2][:, 0:N_OUT]
-                for u in range(2):
-                    j = 2 * c + u
-                    nc.tensor.transpose(part[:, u * P : (u + 1) * P], turned[:, j * P : (j + 1) * P], ident[:])
-            res = sb.tile([P, N_OUT], F32, name=f"res{c}")
-            nc.vector.scalar_tensor_tensor(res[:], f2[:, cols], share_col[:], part, ALU.mult, ALU.add)
+                at = cols.start - GPSIMD_COLUMNS
+                part = banks[at // CHUNK][:, 0:CHUNK]
+                for u in range(CHUNK // P):
+                    nc.tensor.transpose(
+                        part[:, u * P : (u + 1) * P], turned[:, at + u * P : at + (u + 1) * P], ident[:]
+                    )
+            result = sb.tile([P, CHUNK], F32, name=f"result{c}")
+            nc.vector.scalar_tensor_tensor(result[:], f2[:, cols], share_col[:], part, ALU.mult, ALU.add)
             queue = nc.sync if c % 2 == 0 else nc.scalar
-            queue.dma_start(out=out[:, cols], in_=res[:])
+            queue.dma_start(out=out[:, cols], in_=result[:])

import concourse.mybir as mybir
from concourse.masks import make_identity

D, T, SLOTS, Q = 512, 1024, 512, 128
FLOPS = 2 * D * Q * T

F32 = mybir.dt.float32
BF16 = mybir.dt.bfloat16
I32 = mybir.dt.int32
U32 = mybir.dt.uint32
U16 = mybir.dt.uint16
U8 = mybir.dt.uint8
FP8X4 = mybir.dt.float8_e4m3fn_x4
ALU = mybir.AluOpType
ACT = mybir.ActivationFunctionType

P = 128
PACK = 4
QUADRANT = 32
SCALE_ROWS = 4
HEAD = 16
BANKS, BANK_COLUMNS = 8, 512
PLANES = 4
PLANE = T // PLANES
HALF = SLOTS // 2
QUARTER = SLOTS // 4
MATMULS = [(0, 256), (256, 256), (512, 256), (768, 128), (896, 128)]
CHUNK = 256
GPSIMD_COLUMNS = T // 2


def tile_attend_lookahead_lean_twiceput_heads_kernel(
    tc, query, keys_words, keys_scales, lam, old, share2, offs, offs2, offs3, offs4, out
):
    nc = tc.nc
    with tc.tile_pool(name="sb", bufs=1) as sb, tc.psum_pool(name="ps", bufs=1) as ps:
        q_raw = sb.tile([P, PACK, Q], F32, name="q_raw")
        nc.sync.dma_start(out=q_raw[:], in_=query.rearrange("(p j) q -> p j q", j=PACK))

        k_scales = sb.tile([P, PLANE], U8, name="k_scales", align_bytes=64)
        nc.vector.memset(k_scales[:].bitcast(I32), 0)
        words_hbm = keys_words[0].rearrange("p n t -> p (n t)").bitcast(I32)
        k_words = [sb.tile([P, T // 2], I32, name=f"k_words{h}", align_bytes=64) for h in range(2)]
        nc.sync.dma_start(out=k_words[0][:], in_=words_hbm[:, 0 : T // 2])
        for quad in range(P // QUADRANT):
            rows = keys_scales[0, SCALE_ROWS * quad : SCALE_ROWS * (quad + 1), :].bitcast(I32)
            nc.sync.dma_start(
                out=k_scales[QUADRANT * quad : QUADRANT * quad + PLANES * SCALE_ROWS, :].bitcast(I32),
                in_=rows.rearrange("j (c n) -> c j n", c=PLANES),
            )
        nc.sync.dma_start(out=k_words[1][:], in_=words_hbm[:, T // 2 : T])

        def load_list(name, src):
            entries = sb.tile([P, SLOTS // HEAD], U16, name=name)
            nc.sync.dma_start(entries[:], src)
            return entries

        list1 = load_list("list1", offs)
        list3 = load_list("list3", offs3)
        list2 = load_list("list2", offs2)
        lam_col = sb.tile([P, 1], F32, name="lam_col")
        nc.sync.dma_start(out=lam_col[:], in_=lam)
        list4 = load_list("list4", offs4)
        share_col = sb.tile([P, 1], F32, name="share_col")
        nc.sync.dma_start(out=share_col[:], in_=share2)
        old_sb = sb.tile([P, T], F32, name="old_sb")
        nc.sync.dma_start(out=old_sb[:], in_=old)

        f1 = sb.tile([P, T], F32, name="f1")
        f2 = sb.tile([P, T], F32, name="f2")
        nc.vector.memset(f1[:], 0.0)
        warm_in = sb.tile([P, 1], F32, name="warm_in")
        nc.vector.memset(warm_in[:], 0.0)
        warm_out = sb.tile([P, 1], F32, name="warm_out")
        nc.scalar.activation(warm_out[:], warm_in[:], ACT.Sigmoid)
        nc.vector.memset(f2[:], 0.0)

        q_bf = sb.tile([P, Q, PACK], BF16, name="q_bf", align_bytes=64)
        q_codes = sb.tile([P, Q], U32, name="q_codes", align_bytes=64)
        q_scales = sb.tile([P, Q], U8, name="q_scales", align_bytes=64)
        q_halves = [slice(0, Q // 2), slice(Q // 2, Q)]
        for q_cols in q_halves:
            nc.vector.tensor_copy(
                out=q_bf[:, q_cols, :].rearrange("p (c i) j -> p c j i", i=4),
                in_=q_raw[:, :, q_cols].rearrange("p j (c i) -> p c j i", i=4),
            )
        for q_cols in q_halves:
            nc.vector.quantize_mx(
                out=q_codes[:, q_cols].bitcast(FP8X4),
                scales=q_scales[:, q_cols],
                in_=q_bf[:, q_cols, :].rearrange("p q j -> p (q j)"),
            )

        ident = sb.tile([P, P], F32, name="ident")
        make_identity(nc, ident[:])
        banks = [ps.tile([P, BANK_COLUMNS], F32, name=f"bank{b}") for b in range(BANKS)]
        a = sb.tile([P, T], F32, name="a")
        for b, (token, count) in enumerate(MATMULS):
            words_half, word = divmod(token, T // 2)
            plane, plane_col = divmod(token, PLANE)
            sums = banks[b][:, 0:count]
            nc.tensor.matmul_mx(
                out=sums,
                lhsT=q_codes[:].bitcast(FP8X4),
                lhsT_scale=q_scales[:],
                rhs=k_words[words_half][:, word : word + count].bitcast(FP8X4),
                rhs_scale=k_scales[SCALE_ROWS * plane : P, plane_col : plane_col + count],
                start=True,
                stop=True,
            )
            if b % 2 == 0:
                nc.vector.tensor_copy(out=a[:, token : token + count], in_=sums)
            else:
                nc.scalar.activation(a[:, token : token + count], sums, ACT.Copy)

        tensor_blocks = range(GPSIMD_COLUMNS // P, T // P)
        for j in tensor_blocks:
            nc.tensor.matmul(
                banks[j][:, 0:P], old_sb[:, j * P : (j + 1) * P], ident[:], start=True, stop=False, is_transpose=True
            )

        g1 = [sb.tile([P, HALF], F32, name=f"g1_{h}") for h in range(2)]
        g2 = [sb.tile([P, HALF], F32, name=f"g2_{h}") for h in range(2)]
        g3 = [sb.tile([P, HALF], F32, name=f"g3_{h}") for h in range(2)]
        larger = [g1[1], g1[0]]
        s = sb.tile([P, SLOTS], F32, name="s")
        w = sb.tile([P, SLOTS], F32, name="w")

        def offsets(entries, first, last):
            return entries[:, first // HEAD : last // HEAD]

        def looked_up(entries, h):
            return a[:].indirect(offsets(entries, h * HALF, (h + 1) * HALF))

        def weigh(first, last):
            nc.scalar.activation(w[:, first:last], s[:, first:last], ACT.Sigmoid)

        def put(window, entries, first, last):
            nc.vector.tensor_copy(window[:].indirect(offsets(entries, first, last)), w[:, first:last])

        quarters = [slice(0, QUARTER), slice(QUARTER, HALF)]
        nc.scalar.activation(g3[0][:], looked_up(list3, 0), ACT.Copy)
        nc.vector.tensor_copy(g2[0][:], looked_up(list2, 0))
        nc.scalar.activation(g1[0][:], looked_up(list1, 0), ACT.Copy)
        nc.vector.tensor_copy(g2[1][:], looked_up(list2, 1))
        for slots in quarters:
            nc.vector.tensor_tensor(larger[0][:, slots], g2[0][:, slots], g3[0][:, slots], ALU.max)
        nc.scalar.activation(g3[1][:], looked_up(list3, 1), ACT.Copy)
        for slots in quarters:
            nc.vector.scalar_tensor_tensor(
                s[:, slots], larger[0][:, slots], lam_col[:], g1[0][:, slots], ALU.mult, ALU.add
            )
        nc.vector.tensor_tensor(larger[1][:], g2[1][:], g3[1][:], ALU.max)
        for slots in quarters:
            weigh(slots.start, slots.stop)
        nc.scalar.activation(g1[1][:], looked_up(list1, 1), ACT.Copy)
        leaned = sb.tile([P, HALF], F32, name="leaned")
        nc.gpsimd.tensor_scalar(leaned[:], larger[1][:], lam_col[:], 0.0, ALU.mult, ALU.add)
        nc.gpsimd.tensor_tensor(s[:, HALF:], leaned[:], g1[1][:], ALU.add)
        weigh(HALF, SLOTS)

        put(f1, list1, 0, QUARTER)
        put(f2, list4, 0, HALF)
        put(f1, list1, QUARTER, SLOTS)
        put(f2, list4, HALF, SLOTS)

        turned = sb.tile([P, T - GPSIMD_COLUMNS], F32, name="turned")
        for j in tensor_blocks:
            nc.tensor.matmul(
                banks[j][:, 0:P], f1[:, j * P : (j + 1) * P], ident[:], start=False, stop=True, is_transpose=True
            )
            at = j * P - GPSIMD_COLUMNS
            nc.scalar.activation(turned[:, at : at + P], banks[j][:, 0:P], ACT.Copy)
        for c in range(T // CHUNK):
            cols = slice(c * CHUNK, (c + 1) * CHUNK)
            if cols.start < GPSIMD_COLUMNS:
                part_sb = sb.tile([P, CHUNK], F32, name=f"part{c}")
                part = part_sb[:]
                nc.gpsimd.tensor_tensor(part, old_sb[:, cols], f1[:, cols], ALU.add)
            else:
                at = cols.start - GPSIMD_COLUMNS
                part = banks[at // CHUNK][:, 0:CHUNK]
                for u in range(CHUNK // P):
                    nc.tensor.transpose(
                        part[:, u * P : (u + 1) * P], turned[:, at + u * P : at + (u + 1) * P], ident[:]
                    )
            result = sb.tile([P, CHUNK], F32, name=f"result{c}")
            nc.vector.scalar_tensor_tensor(result[:], f2[:, cols], share_col[:], part, ALU.mult, ALU.add)
            queue = nc.sync if c % 2 == 0 else nc.scalar
            queue.dma_start(out=out[:, cols], in_=result[:])
